import numpy as np
import ml_dtypes


def mxq(x, axis, fmt="e4m3"):
    dtype, down = {"e4m3": (ml_dtypes.float8_e4m3fn, 7), "e5m2": (ml_dtypes.float8_e5m2, 14)}[fmt]
    v = np.moveaxis(np.asarray(x, np.float32).astype(ml_dtypes.bfloat16).astype(np.float64), axis, -1)
    blocks = v.reshape(v.shape[:-1] + (-1, 32))
    amax = np.abs(blocks).max(-1, keepdims=True)
    byte = np.maximum(np.where(amax > 0, np.frexp(amax)[1] - 1 + 127, 0) - down, 1)
    scale = np.exp2(byte - 127.0)
    codes = (blocks / scale).astype(np.float32).astype(dtype).astype(np.float64)
    return np.moveaxis((codes * scale).reshape(v.shape), -1, axis)


WIDE = False


def mx_kscale(k):
    if not WIDE:
        return np.ones(k)
    levels = np.array([10, -10, 5, -5, 0])
    if k % 512:
        return np.exp2(np.random.permutation(np.resize(levels, k // 32))).repeat(32)
    a = np.empty((k // 512, 16))
    for p in range(k // 512):
        a[p, :8] = np.random.permutation(np.resize(levels, 8))
        for g in range(8):
            far = levels[np.abs(levels - a[p, g]) >= 10]
            a[p, g + 8] = far[np.random.randint(len(far))]
    return np.exp2(a.ravel()).repeat(32)


def f64(x):
    return np.asarray(x).astype(np.float64)


def striped(idx):
    return np.tile(idx.reshape(-1, 16).T, (8, 1)).astype(np.uint16)


def unstriped(offs):
    return offs[:16].T.reshape(-1).astype(np.int64)


def pack_weight(w):
    k, n = w.shape
    w = f64(np.asarray(w, np.float32).astype(ml_dtypes.bfloat16)).reshape(k // 32, 32, n)
    amax = np.abs(w).max(1)
    byte = np.clip(np.where(amax > 0, np.frexp(amax)[1] - 1 + 127 - 7, 1), 1, 254)
    scaled = (w * np.exp2(127.0 - byte)[:, None, :]).reshape(k, n).astype(np.float32)
    words = np.ascontiguousarray(scaled.reshape(k // 512, 128, 4, n).transpose(0, 1, 3, 2)).astype(ml_dtypes.float8_e4m3fn).view(np.uint8)
    return words, np.ascontiguousarray(byte.astype(np.uint8).reshape(k // 512, 16, n))


def unpack_weight(words, scales):
    g, p, n, _ = words.shape
    vals = np.ascontiguousarray(words).view(ml_dtypes.float8_e4m3fn).astype(np.float64) * np.repeat(np.exp2(scales.astype(np.float64) - 127.0), 8, axis=1)[..., None]
    return vals.transpose(0, 1, 3, 2).reshape(g * 512, n)


K, T, S, N, H = 1024, 2048, 512, 128, 512


def setup_inputs():
    n = np.random.standard_normal
    s = mx_kscale(K)[:, None]
    u = mx_kscale(H)
    packed_xT = pack_weight(n((K, T)) * s)
    return {
        "x_words": packed_xT[0],
        "x_scales": packed_xT[1],
        "w1": (n((K, H)) / np.sqrt(K) / s).astype(np.float32),
        "unit": (np.random.uniform(0.6, 1.4, (H, 1)) * u[:, None]).astype(np.float32),
        "w2": (n((H, N)) / np.sqrt(H) / u[:, None]).astype(np.float32),
        "offs": striped(np.random.permutation(T)[:S]),
        "p1": striped(np.random.permutation(S)),
        "p2": striped(np.random.permutation(S)),
        "p3": striped(np.random.permutation(S)),
    }


def reference(x_words, x_scales, w1, unit, w2, offs, p1, p2, p3):
    xq = unpack_weight(x_words, x_scales)[:, unstriped(offs)]
    y = mxq(f64(w1), 0, "e4m3").T @ xq
    y2 = (y) ** 2
    ms = y2.mean(axis=1, keepdims=True)
    nrm = y / np.sqrt(ms + 0.1)
    a1 = nrm[:, unstriped(p1)]
    a2 = nrm[:, unstriped(p2)]
    a3 = nrm[:, unstriped(p3)]
    sum3 = a1 + a2 + a3
    mxp = np.maximum(np.maximum(a1, a2), a3)
    mnp = np.minimum(np.minimum(a1, a2), a3)
    med = sum3 - mxp - mnp
    hid = f64(unit) * (0.5 * nrm + med)
    return mxq(f64(w2), 0, "e4m3").T @ mxq(hid, 0, "e4m3")

@@ -1,0 +1,223 @@
+from contextlib import ExitStack
+
+import concourse.mybir as mybir
+
+K, T, S, N, H = 1024, 2048, 512, 128, 512
+FLOPS = 2 * K * H * S + 2 * H * N * S
+
+F32 = mybir.dt.float32
+BF16 = mybir.dt.bfloat16
+I32 = mybir.dt.int32
+U32 = mybir.dt.uint32
+U16 = mybir.dt.uint16
+U8 = mybir.dt.uint8
+FP8X4 = mybir.dt.float8_e4m3fn_x4
+ALU = mybir.AluOpType
+ACT = mybir.ActivationFunctionType
+
+P = 128
+PACK = 4
+K_PASS = P * PACK
+PASSES = K // K_PASS
+WINDOW = 704
+HALF = S // 2
+LIST_ROWS = 16
+EPS = 0.1
+
+
+def tile_picked_ygossip_med_p_kernel(
+    tc, x_words, x_scales, w1, unit, w2, offs, p1, p2, p3, out
+):
+    nc = tc.nc
+    with ExitStack() as ctx:
+        sb = ctx.enter_context(tc.tile_pool(name="sb", bufs=1))
+        ps = ctx.enter_context(tc.psum_pool(name="ps", bufs=1))
+
+        def tiles(name, count, shape, dtype):
+            return [sb.tile(shape, dtype, name=f"{name}{i}", align_bytes=64) for i in range(count)]
+
+        lists = tiles("list", 4, [P, S // LIST_ROWS], U16)
+        w1_raw = tiles("w1_raw", PASSES, [P, PACK, H], F32)
+        table = tiles("table", PASSES, [P, T], U32)
+        table_scales = sb.tile([P, T], U8, align_bytes=64, tag="shared")
+        gain = tiles("gain", PACK, [P, 1], F32)
+        w2_raw = sb.tile([P, PACK, N], F32, align_bytes=64)
+        z = tiles("z", PACK, [P, WINDOW], F32)
+        minus_half = sb.tile([P, 1], F32)
+
+        nc.vector.memset(table_scales[:].bitcast(I32), 0)
+        for quad in range(4):
+            nc.gpsimd.dma_start(
+                out=table_scales[32 * quad : 32 * quad + 4 * PASSES, :].bitcast(I32),
+                in_=x_scales[:, 4 * quad : 4 * quad + 4, :].bitcast(I32),
+            )
+        nc.gpsimd.memset(minus_half[:], -0.5)
+        for t in range(PACK):
+            nc.vector.memset(z[t][:, S:], 0.0)
+
+        for g in range(PASSES):
+            nc.sync.dma_start(
+                out=w1_raw[g][:], in_=w1[g * K_PASS : (g + 1) * K_PASS, :].rearrange("(p j) n -> p j n", j=PACK)
+            )
+        nc.sync.dma_start(lists[0][:], offs)
+        for g in range(PASSES):
+            nc.sync.dma_start(
+                out=table[g][:].bitcast(I32), in_=x_words[g].rearrange("p n r -> p (n r)").bitcast(I32)
+            )
+        for dst, src in zip(lists[1:], (p1, p2, p3)):
+            nc.sync.dma_start(dst[:], src)
+        w2_rows = w2.rearrange("(q t c) n -> t q c n", t=PACK, c=4)
+        unit_rows = unit.rearrange("(q t c) o -> t q c o", t=PACK, c=4)
+        with nc.allow_non_contiguous_dma(reason="one gain value a partition"):
+            nc.sync.dma_start(out=gain[0][:], in_=unit_rows[0])
+        for t in range(PACK):
+            nc.sync.dma_start(out=w2_raw[:, t, :], in_=w2_rows[t])
+        with nc.allow_non_contiguous_dma(reason="one gain value a partition"):
+            for t in range(1, PACK):
+                nc.sync.dma_start(out=gain[t][:], in_=unit_rows[t])
+
+        w1_codes = tiles("w1_codes", 2 * PASSES, [P, 2 * P], U32)
+        w1_scales = tiles("w1_scales", 2 * PASSES, [P, 2 * P], U8)
+        w1_bf = tiles("w1_bf", 2 * PASSES, [P, 2 * P * PACK], BF16)
+        for g in range(PASSES):
+            src = w1_raw[g][:].rearrange("p j (q t c) -> p q t j c", t=PACK, c=4)
+            for pair, copy in enumerate((nc.vector.tensor_copy, nc.scalar.copy)):
+                copy(
+                    out=w1_bf[2 * g + pair][:].rearrange("p (t q c j) -> p q t j c", t=2, c=4, j=PACK),
+                    in_=src[:, :, 2 * pair : 2 * pair + 2],
+                )
+            for pair in range(2):
+                i = 2 * g + pair
+                nc.vector.quantize_mx(out=w1_codes[i][:].bitcast(FP8X4), scales=w1_scales[i][:], in_=w1_bf[i][:])
+
+        picked_scales = sb.tile([P, S], U8, align_bytes=64)
+        nc.vector.tensor_copy(picked_scales[:], table_scales[:].indirect(lists[0][:]))
+        picked = [
+            sb.tile([P, S], U32, name="picked0", align_bytes=64, tag="shared"),
+            sb.tile([P, S], U32, name="picked1", align_bytes=64),
+        ]
+        y = [ps.tile([P, S], F32, name=f"y{t}") for t in range(PACK)]
+        for g in range(PASSES):
+            nc.vector.tensor_copy(picked[g][:], table[g][:].indirect(lists[0][:]))
+            for t in range(PACK):
+                i = 2 * g + t // 2
+                cols = slice((t % 2) * P, (t % 2 + 1) * P)
+                nc.tensor.matmul_mx(
+                    out=y[t][:],
+                    lhsT=w1_codes[i][:, cols].bitcast(FP8X4),
+                    lhsT_scale=w1_scales[i][:, cols],
+                    rhs=picked[g][:].bitcast(FP8X4),
+                    rhs_scale=picked_scales[4 * g :, :],
+                    start=(g == 0),
+                    stop=(g == PASSES - 1),
+                )
+
+        w2_bf = sb.tile([P, N * PACK], BF16, align_bytes=64)
+        w2_codes = sb.tile([P, N], U32, align_bytes=64)
+        w2_scales = sb.tile([P, N], U8, align_bytes=64)
+
+        def prepare_w2():
+            nc.vector.tensor_copy(
+                out=w2_bf[:].rearrange("p (a c t) -> p a t c", c=4, t=PACK),
+                in_=w2_raw[:].rearrange("p t (a c) -> p a t c", c=4),
+            )
+
+        def quantise_w2():
+            nc.vector.quantize_mx(out=w2_codes[:].bitcast(FP8X4), scales=w2_scales[:], in_=w2_bf[:])
+
+        squares = tiles("squares", PACK, [P, S], BF16)
+        total = tiles("total", PACK, [P, 1], F32)
+        mean = tiles("mean", PACK, [P, 1], F32)
+        rstd = tiles("rstd", PACK, [P, 1], F32)
+        a1 = tiles("a1_", PACK, [P, S], F32)
+        a2 = tiles("a2_", PACK, [P, S], F32)
+        a3 = tiles("a3_", PACK, [P, S], F32)
+        low = tiles("low", PACK, [P, S], F32)
+        high = tiles("high", PACK, [P, S], F32)
+        capped = tiles("capped", PACK, [P, S], F32)
+        median = tiles("median", PACK, [P, S], F32)
+        hid = sb.tile([P, PACK, S], F32, align_bytes=64)
+        halves = [slice(0, HALF), slice(HALF, S)]
+        whole = slice(0, S)
+
+        def row_norm(t):
+            nc.scalar.activation(out=squares[t][:], in_=y[t][:], func=ACT.Square, accum_out=total[t][:])
+            nc.gpsimd.tensor_scalar(mean[t][:], total[t][:], 1.0 / S, EPS, ALU.mult, ALU.add)
+            nc.gpsimd.tensor_tensor(rstd[t][:], mean[t][:], minus_half[:], ALU.pow)
+
+        def scale_out(t):
+            nc.vector.tensor_scalar(z[t][:, :S], y[t][:], rstd[t][:], gain[t][:], ALU.mult, ALU.mult)
+
+        def partners(t, which, cols):
+            return z[t][:].indirect(lists[which][:, cols.start // LIST_ROWS : cols.stop // LIST_ROWS])
+
+        def fetch_scalar(dst, t, which, cols):
+            nc.scalar.activation(out=dst[t][:, cols], in_=partners(t, which, cols), func=ACT.Copy)
+
+        def order_two(t, cols):
+            nc.vector.tensor_tensor(high[t][:, cols], a1[t][:, cols], a2[t][:, cols], ALU.max)
+            nc.vector.tensor_tensor(low[t][:, cols], a1[t][:, cols], a2[t][:, cols], ALU.min)
+
+        def finish(t, cols):
+            mid = (cols.start + cols.stop) // 2
+            parts = [slice(cols.start, mid), slice(mid, cols.stop)]
+            for c in parts:
+                nc.vector.tensor_tensor(capped[t][:, c], high[t][:, c], a3[t][:, c], ALU.min)
+            for c in parts:
+                nc.vector.tensor_tensor(median[t][:, c], capped[t][:, c], low[t][:, c], ALU.max)
+            for c in parts:
+                nc.vector.scalar_tensor_tensor(hid[:, t, c], z[t][:, c], 0.5, median[t][:, c], ALU.mult, ALU.add)
+
+        row_norm(0)
+        prepare_w2()
+        row_norm(1)
+        scale_out(0)
+        quantise_w2()
+        row_norm(2)
+        fetch_scalar(a1, 0, 1, whole)
+        nc.vector.tensor_copy(a2[0][:], partners(0, 2, whole))
+        fetch_scalar(a3, 0, 3, whole)
+        scale_out(1)
+        row_norm(3)
+        order_two(0, whole)
+        finish(0, whole)
+        for t in (1, 2):
+            fetch_scalar(a1, t, 1, whole)
+            fetch_scalar(a2, t, 2, whole)
+            fetch_scalar(a3, t, 3, whole)
+            scale_out(t + 1)
+            order_two(t, whole)
+            finish(t, whole)
+        last = PACK - 1
+        for cols in halves:
+            fetch_scalar(a1, last, 1, cols)
+            fetch_scalar(a2, last, 2, cols)
+            fetch_scalar(a3, last, 3, cols)
+            order_two(last, cols)
+            finish(last, cols)
+
+        hid_bf = tiles("hid_bf", 2, [P, HALF * PACK], BF16)
+        hid_codes = tiles("hid_codes", 2, [P, HALF], U32)
+        hid_scales = tiles("hid_scales", 2, [P, HALF], U8)
+        result = tiles("result", 2, [P, HALF], F32)
+        acc = [ps.tile([P, HALF], F32, name=f"acc{i}") for i in range(2)]
+        movers = (nc.scalar.copy, nc.vector.tensor_copy)
+        for i, cols in enumerate(halves):
+            movers[i](
+                out=hid_bf[i][:].rearrange("p (a c t) -> p a t c", c=4, t=PACK),
+                in_=hid[:, :, cols].rearrange("p t (a c) -> p a t c", c=4),
+            )
+        for i, cols in enumerate(halves):
+            nc.vector.quantize_mx(out=hid_codes[i][:].bitcast(FP8X4), scales=hid_scales[i][:], in_=hid_bf[i][:])
+            nc.tensor.matmul_mx(
+                out=acc[i][:],
+                lhsT=w2_codes[:].bitcast(FP8X4),
+                lhsT_scale=w2_scales[:],
+                rhs=hid_codes[i][:].bitcast(FP8X4),
+                rhs_scale=hid_scales[i][:],
+                start=True,
+                stop=True,
+            )
+        for i, cols in enumerate(halves):
+            movers[i](out=result[i][:], in_=acc[i][:])
+            nc.sync.dma_start(out=out[:, cols], in_=result[i][:])

@@ -37,80 +37,115 @@ def tile_picked_ygossip_med_p_kernel(
             return [sb.tile(shape, dtype, name=f"{name}{i}", align_bytes=64) for i in range(count)]
 
         lists = tiles("list", 4, [P, S // LIST_ROWS], U16)
-        w1_raw = tiles("w1_raw", PASSES, [P, PACK, H], F32)
+        w1_raw = [tiles(f"w1_raw{h}_", PASSES, [P, PACK, H // 2], F32) for h in range(2)]
         table = tiles("table", PASSES, [P, T], U32)
+        scale_rows = sb.tile([P, T // 4], I32, align_bytes=64)
         table_scales = sb.tile([P, T], U8, align_bytes=64, tag="shared")
         gain = tiles("gain", PACK, [P, 1], F32)
         w2_raw = sb.tile([P, PACK, N], F32, align_bytes=64)
         z = tiles("z", PACK, [P, WINDOW], F32)
-        minus_half = sb.tile([P, 1], F32)
 
-        nc.vector.memset(table_scales[:].bitcast(I32), 0)
         for quad in range(4):
-            nc.gpsimd.dma_start(
-                out=table_scales[32 * quad : 32 * quad + 4 * PASSES, :].bitcast(I32),
+            nc.sync.dma_start(
+                out=scale_rows[32 * quad : 32 * quad + 4 * PASSES, :],
                 in_=x_scales[:, 4 * quad : 4 * quad + 4, :].bitcast(I32),
             )
-        nc.gpsimd.memset(minus_half[:], -0.5)
+        nc.vector.memset(table_scales[:].bitcast(I32), 0)
         for t in range(PACK):
             nc.vector.memset(z[t][:, S:], 0.0)
 
-        for g in range(PASSES):
-            nc.sync.dma_start(
-                out=w1_raw[g][:], in_=w1[g * K_PASS : (g + 1) * K_PASS, :].rearrange("(p j) n -> p j n", j=PACK)
-            )
+        w2_rows = w2.rearrange("(q t c) n -> t q c n", t=PACK, c=4)
+        unit_rows = unit.rearrange("(q t c) o -> t q c o", t=PACK, c=4)
+
+        def load_w1(h):
+            for g in range(PASSES):
+                rows = w1[g * K_PASS : (g + 1) * K_PASS, h * (H // 2) : (h + 1) * (H // 2)]
+                nc.sync.dma_start(out=w1_raw[h][g][:], in_=rows.rearrange("(p j) n -> p j n", j=PACK))
+
+        def load_gain(i):
+            with nc.allow_non_contiguous_dma(reason="one gain value a partition"):
+                if i < 2:
+                    for t in range(2):
+                        nc.sync.dma_start(
+                            out=gain[i][64 * t : 64 * t + 64, :], in_=unit_rows[t, 16 * i : 16 * i + 16]
+                        )
+                else:
+                    nc.sync.dma_start(out=gain[i][:], in_=unit_rows[i])
+
+        load_w1(0)
         nc.sync.dma_start(lists[0][:], offs)
         for g in range(PASSES):
             nc.sync.dma_start(
                 out=table[g][:].bitcast(I32), in_=x_words[g].rearrange("p n r -> p (n r)").bitcast(I32)
             )
+        load_gain(0)
         for dst, src in zip(lists[1:], (p1, p2, p3)):
             nc.sync.dma_start(dst[:], src)
-        w2_rows = w2.rearrange("(q t c) n -> t q c n", t=PACK, c=4)
-        unit_rows = unit.rearrange("(q t c) o -> t q c o", t=PACK, c=4)
-        with nc.allow_non_contiguous_dma(reason="one gain value a partition"):
-            nc.sync.dma_start(out=gain[0][:], in_=unit_rows[0])
+        load_w1(1)
+        for i in range(1, PACK):
+            load_gain(i)
         for t in range(PACK):
             nc.sync.dma_start(out=w2_raw[:, t, :], in_=w2_rows[t])
-        with nc.allow_non_contiguous_dma(reason="one gain value a partition"):
-            for t in range(1, PACK):
-                nc.sync.dma_start(out=gain[t][:], in_=unit_rows[t])
 
-        w1_codes = tiles("w1_codes", 2 * PASSES, [P, 2 * P], U32)
-        w1_scales = tiles("w1_scales", 2 * PASSES, [P, 2 * P], U8)
-        w1_bf = tiles("w1_bf", 2 * PASSES, [P, 2 * P * PACK], BF16)
-        for g in range(PASSES):
-            src = w1_raw[g][:].rearrange("p j (q t c) -> p q t j c", t=PACK, c=4)
-            for pair, copy in enumerate((nc.vector.tensor_copy, nc.scalar.copy)):
-                copy(
-                    out=w1_bf[2 * g + pair][:].rearrange("p (t q c j) -> p q t j c", t=2, c=4, j=PACK),
-                    in_=src[:, :, 2 * pair : 2 * pair + 2],
-                )
-            for pair in range(2):
-                i = 2 * g + pair
-                nc.vector.quantize_mx(out=w1_codes[i][:].bitcast(FP8X4), scales=w1_scales[i][:], in_=w1_bf[i][:])
+        for quad in range(4):
+            rows = slice(32 * quad, 32 * quad + 4 * PASSES)
+            nc.vector.tensor_copy(table_scales[rows, :].bitcast(I32), scale_rows[rows, :])
+
+        w1_bf = [tiles(f"w1_bf{h}_", PASSES, [P, PACK * H // 2], BF16) for h in range(2)]
+        early_codes = [tiles(f"early_codes{h}_", PASSES, [P, P], U32) for h in range(2)]
+        early_scales = [tiles(f"early_scales{h}_", PASSES, [P, P], U8) for h in range(2)]
+        late_codes = tiles("late_codes", PASSES, [P, 2 * P], U32)
+        late_scales = tiles("late_scales", PASSES, [P, 2 * P], U8)
+
+        def round_w1(copy, h, g):
+            copy(
+                out=w1_bf[h][g][:].rearrange("p (t q c j) -> p q t j c", t=PACK, c=4, j=PACK),
+                in_=w1_raw[h][g][:].rearrange("p j (q t c) -> p q t j c", t=PACK, c=4),
+            )
+
+        def quantise_early(h, g):
+            quantise(early_codes[h][g], early_scales[h][g], w1_bf[h][g][:, : 2 * 256])
+
+        def quantise_late(h, g):
+            for t in (2, 3):
+                cols = slice((t - 2) * P + 64 * h, (t - 2) * P + 64 * h + 64)
+                quantise(late_codes[g][:, cols], late_scales[g][:, cols], w1_bf[h][g][:, 256 * t : 256 * t + 256])
+
+        def quantise(codes, scales, values):
+            nc.vector.quantize_mx(out=codes[:].bitcast(FP8X4), scales=scales[:], in_=values)
 
         picked_scales = sb.tile([P, S], U8, align_bytes=64)
+        y = [ps.tile([P, S], F32, name=f"y{t}") for t in range(PACK)]
+
+        def product(i, g):
+            if i < 2:
+                codes, scales = early_codes[i][g][:], early_scales[i][g][:]
+            else:
+                cols = slice((i - 2) * P, (i - 1) * P)
+                codes, scales = late_codes[g][:, cols], late_scales[g][:, cols]
+            nc.tensor.matmul_mx(
+                out=y[i][:],
+                lhsT=codes.bitcast(FP8X4),
+                lhsT_scale=scales,
+                rhs=picked[g][:].bitcast(FP8X4),
+                rhs_scale=picked_scales[4 * g :, :],
+                start=(g == 0),
+                stop=(g == PASSES - 1),
+            )
+
+        for g in range(PASSES):
+            round_w1(nc.vector.tensor_copy, 0, g)
+        for g in range(PASSES):
+            quantise_early(0, g)
+            quantise_late(0, g)
         nc.vector.tensor_copy(picked_scales[:], table_scales[:].indirect(lists[0][:]))
         picked = [
             sb.tile([P, S], U32, name="picked0", align_bytes=64, tag="shared"),
             sb.tile([P, S], U32, name="picked1", align_bytes=64),
         ]
-        y = [ps.tile([P, S], F32, name=f"y{t}") for t in range(PACK)]
         for g in range(PASSES):
             nc.vector.tensor_copy(picked[g][:], table[g][:].indirect(lists[0][:]))
-            for t in range(PACK):
-                i = 2 * g + t // 2
-                cols = slice((t % 2) * P, (t % 2 + 1) * P)
-                nc.tensor.matmul_mx(
-                    out=y[t][:],
-                    lhsT=w1_codes[i][:, cols].bitcast(FP8X4),
-                    lhsT_scale=w1_scales[i][:, cols],
-                    rhs=picked[g][:].bitcast(FP8X4),
-                    rhs_scale=picked_scales[4 * g :, :],
-                    start=(g == 0),
-                    stop=(g == PASSES - 1),
-                )
+            product(0, g)
 
         w2_bf = sb.tile([P, N * PACK], BF16, align_bytes=64)
         w2_codes = sb.tile([P, N], U32, align_bytes=64)
@@ -127,7 +162,9 @@ def tile_picked_ygossip_med_p_kernel(
 
         squares = tiles("squares", PACK, [P, S], BF16)
         total = tiles("total", PACK, [P, 1], F32)
-        mean = tiles("mean", PACK, [P, 1], F32)
+        stats = sb.tile([P, 6], F32)
+        moments = sb.tile([P, 2], F32)
+        staged = sb.tile([P, S], F32, align_bytes=64)
         rstd = tiles("rstd", PACK, [P, 1], F32)
         a1 = tiles("a1_", PACK, [P, S], F32)
         a2 = tiles("a2_", PACK, [P, S], F32)
@@ -140,10 +177,13 @@ def tile_picked_ygossip_med_p_kernel(
         halves = [slice(0, HALF), slice(HALF, S)]
         whole = slice(0, S)
 
-        def row_norm(t):
+        def sum_squares(t):
             nc.scalar.activation(out=squares[t][:], in_=y[t][:], func=ACT.Square, accum_out=total[t][:])
-            nc.gpsimd.tensor_scalar(mean[t][:], total[t][:], 1.0 / S, EPS, ALU.mult, ALU.add)
-            nc.gpsimd.tensor_tensor(rstd[t][:], mean[t][:], minus_half[:], ALU.pow)
+
+        def take_root(t, scale):
+            nc.scalar.activation(
+                out=rstd[t][:], in_=total[t][:], func=ACT.Abs_reciprocal_sqrt, scale=scale, bias=EPS
+            )
 
         def scale_out(t):
             nc.vector.tensor_scalar(z[t][:, :S], y[t][:], rstd[t][:], gain[t][:], ALU.mult, ALU.mult)
@@ -158,36 +198,71 @@ def tile_picked_ygossip_med_p_kernel(
             nc.vector.tensor_tensor(high[t][:, cols], a1[t][:, cols], a2[t][:, cols], ALU.max)
             nc.vector.tensor_tensor(low[t][:, cols], a1[t][:, cols], a2[t][:, cols], ALU.min)
 
+        def cap(t, c):
+            nc.vector.tensor_tensor(capped[t][:, c], high[t][:, c], a3[t][:, c], ALU.min)
+
+        def lift(t, c):
+            nc.vector.tensor_tensor(median[t][:, c], capped[t][:, c], low[t][:, c], ALU.max)
+
+        def mix(t, c):
+            dst = staged[:, c] if t == 1 else hid[:, t, c]
+            nc.vector.scalar_tensor_tensor(dst, z[t][:, c], 0.5, median[t][:, c], ALU.mult, ALU.add)
+
         def finish(t, cols):
             mid = (cols.start + cols.stop) // 2
-            parts = [slice(cols.start, mid), slice(mid, cols.stop)]
-            for c in parts:
-                nc.vector.tensor_tensor(capped[t][:, c], high[t][:, c], a3[t][:, c], ALU.min)
-            for c in parts:
-                nc.vector.tensor_tensor(median[t][:, c], capped[t][:, c], low[t][:, c], ALU.max)
-            for c in parts:
-                nc.vector.scalar_tensor_tensor(hid[:, t, c], z[t][:, c], 0.5, median[t][:, c], ALU.mult, ALU.add)
+            for step in (cap, lift, mix):
+                step(t, slice(cols.start, mid))
+                step(t, slice(mid, cols.stop))
 
-        row_norm(0)
-        prepare_w2()
-        row_norm(1)
+        round_w1(nc.vector.tensor_copy, 1, 0)
+        nc.vector.bn_stats(stats[:], y[0][:])
+        quantise_early(1, 0)
+        product(1, 0)
+        nc.vector.bn_aggr(moments[:], stats[:])
+        nc.vector.scalar_tensor_tensor(
+            total[0][:], moments[:, 0:1], moments[:, 0:1], moments[:, 1:2], ALU.mult, ALU.add
+        )
+        take_root(0, 1.0)
+        quantise_late(1, 0)
         scale_out(0)
-        quantise_w2()
-        row_norm(2)
+        round_w1(nc.scalar.copy, 1, 1)
         fetch_scalar(a1, 0, 1, whole)
+        quantise_early(1, 1)
+        product(1, 1)
+        quantise_late(1, 1)
+        for i in (2, 3):
+            for g in range(PASSES):
+                product(i, g)
         nc.vector.tensor_copy(a2[0][:], partners(0, 2, whole))
+        sum_squares(1)
+        take_root(1, 1.0 / S)
         fetch_scalar(a3, 0, 3, whole)
         scale_out(1)
-        row_norm(3)
         order_two(0, whole)
         finish(0, whole)
-        for t in (1, 2):
-            fetch_scalar(a1, t, 1, whole)
-            fetch_scalar(a2, t, 2, whole)
-            fetch_scalar(a3, t, 3, whole)
-            scale_out(t + 1)
-            order_two(t, whole)
-            finish(t, whole)
+        nc.sync.dma_start(out=hid[0:64, 1, :], in_=hid[64:128, 0, :])
+        fetch_scalar(a1, 1, 1, whole)
+        fetch_scalar(a2, 1, 2, whole)
+        sum_squares(2)
+        take_root(2, 1.0 / S)
+        fetch_scalar(a3, 1, 3, whole)
+        order_two(1, whole)
+        scale_out(2)
+        cap(1, whole)
+        prepare_w2()
+        lift(1, whole)
+        quantise_w2()
+        mix(1, whole)
+        nc.sync.dma_start(out=hid[64:128, 0, :], in_=staged[0:64, :])
+        nc.sync.dma_start(out=hid[64:128, 1, :], in_=staged[64:128, :])
+        fetch_scalar(a1, 2, 1, whole)
+        sum_squares(3)
+        take_root(3, 1.0 / S)
+        fetch_scalar(a2, 2, 2, whole)
+        fetch_scalar(a3, 2, 3, whole)
+        scale_out(3)
+        order_two(2, whole)
+        finish(2, whole)
         last = PACK - 1
         for cols in halves:
             fetch_scalar(a1, last, 1, cols)
@@ -202,11 +277,16 @@ def tile_picked_ygossip_med_p_kernel(
         result = tiles("result", 2, [P, HALF], F32)
         acc = [ps.tile([P, HALF], F32, name=f"acc{i}") for i in range(2)]
         movers = (nc.scalar.copy, nc.vector.tensor_copy)
-        for i, cols in enumerate(halves):
-            movers[i](
-                out=hid_bf[i][:].rearrange("p (a c t) -> p a t c", c=4, t=PACK),
-                in_=hid[:, :, cols].rearrange("p t (a c) -> p a t c", c=4),
+
+        def interleave(copy, i, first, count):
+            copy(
+                out=hid_bf[i][:, PACK * first : PACK * (first + count)].rearrange("p (a c t) -> p a t c", c=4, t=PACK),
+                in_=hid[:, :, i * HALF + first : i * HALF + first + count].rearrange("p t (a c) -> p a t c", c=4),
             )
+
+        interleave(nc.scalar.copy, 0, 0, HALF)
+        interleave(nc.vector.tensor_copy, 1, 0, 160)
+        interleave(nc.scalar.copy, 1, 160, HALF - 160)
         for i, cols in enumerate(halves):
             nc.vector.quantize_mx(out=hid_codes[i][:].bitcast(FP8X4), scales=hid_scales[i][:], in_=hid_bf[i][:])
             nc.tensor.matmul_mx(

@@ -17,11 +17,17 @@ ACT = mybir.ActivationFunctionType
 
 P = 128
 PACK = 4
+RUN = 4
 K_PASS = P * PACK
 PASSES = K // K_PASS
-WINDOW = 704
-HALF = S // 2
+QUADRANT = 32
+SCALE_ROWS = 4
 LIST_ROWS = 16
+HALF_P = P // 2
+HALF_H = H // 2
+HALF_S = S // 2
+WINDOW = 704
+SCALAR_TOKENS = 192
 EPS = 0.1
 
 
@@ -33,271 +39,232 @@ def tile_picked_ygossip_med_p_kernel(
         sb = ctx.enter_context(tc.tile_pool(name="sb", bufs=1))
         ps = ctx.enter_context(tc.psum_pool(name="ps", bufs=1))
 
-        def tiles(name, count, shape, dtype):
-            return [sb.tile(shape, dtype, name=f"{name}{i}", align_bytes=64) for i in range(count)]
+        def tile(name, shape, dtype, tag=None):
+            return sb.tile(shape, dtype, name=name, tag=tag or name, align_bytes=64)
 
-        lists = tiles("list", 4, [P, S // LIST_ROWS], U16)
-        w1_raw = [tiles(f"w1_raw{h}_", PASSES, [P, PACK, H // 2], F32) for h in range(2)]
+        def tiles(name, count, shape, dtype):
+            return [tile(f"{name}{i}", shape, dtype) for i in range(count)]
+
+        def quantise(codes, scales, values):
+            nc.vector.quantize_mx(out=codes.bitcast(FP8X4), scales=scales, in_=values)
+
+        pick_list = tile("pick_list", [P, S // LIST_ROWS], U16)
+        partner_lists = tiles("partner_list", 3, [P, S // LIST_ROWS], U16)
+        w1_raw = [tiles(f"w1_raw{h}_", PASSES, [P, PACK, HALF_H], F32) for h in range(2)]
         table = tiles("table", PASSES, [P, T], U32)
-        scale_rows = sb.tile([P, T // 4], I32, align_bytes=64)
-        table_scales = sb.tile([P, T], U8, align_bytes=64, tag="shared")
+        scale_rows = tile("scale_rows", [P, T // 4], I32)
+        table_scales = tile("table_scales", [P, T], U8)
         gain = tiles("gain", PACK, [P, 1], F32)
-        w2_raw = sb.tile([P, PACK, N], F32, align_bytes=64)
+        w2_raw = tile("w2_raw", [P, PACK, N], F32)
         z = tiles("z", PACK, [P, WINDOW], F32)
 
-        for quad in range(4):
-            nc.sync.dma_start(
-                out=scale_rows[32 * quad : 32 * quad + 4 * PASSES, :],
-                in_=x_scales[:, 4 * quad : 4 * quad + 4, :].bitcast(I32),
-            )
+        live_rows = [slice(QUADRANT * quad, QUADRANT * quad + SCALE_ROWS * PASSES) for quad in range(4)]
+        for quad, queue in enumerate((nc.sync, nc.sync, nc.sync, nc.sync)):
+            rows = x_scales[:, SCALE_ROWS * quad : SCALE_ROWS * (quad + 1), :]
+            queue.dma_start(out=scale_rows[live_rows[quad], :], in_=rows.bitcast(I32))
         nc.vector.memset(table_scales[:].bitcast(I32), 0)
         for t in range(PACK):
             nc.vector.memset(z[t][:, S:], 0.0)
 
-        w2_rows = w2.rearrange("(q t c) n -> t q c n", t=PACK, c=4)
-        unit_rows = unit.rearrange("(q t c) o -> t q c o", t=PACK, c=4)
+        warm_up = tile("warm_up", [P, 1], F32)
+        nc.scalar.activation(out=warm_up[:], in_=z[0][:, S : S + 1], func=ACT.Abs_reciprocal_sqrt, bias=EPS)
 
-        def load_w1(h):
-            for g in range(PASSES):
-                rows = w1[g * K_PASS : (g + 1) * K_PASS, h * (H // 2) : (h + 1) * (H // 2)]
-                nc.sync.dma_start(out=w1_raw[h][g][:], in_=rows.rearrange("(p j) n -> p j n", j=PACK))
+        w2_rows = w2.rearrange("(q t c) n -> t q c n", t=PACK, c=RUN)
+        unit_rows = unit.rearrange("(q t c) o -> t q c o", t=PACK, c=RUN)
+
+        def load_w1(h, g):
+            rows = w1[g * K_PASS : (g + 1) * K_PASS, h * HALF_H : (h + 1) * HALF_H]
+            nc.sync.dma_start(out=w1_raw[h][g][:], in_=rows.rearrange("(p j) n -> p j n", j=PACK))
 
         def load_gain(i):
-            with nc.allow_non_contiguous_dma(reason="one gain value a partition"):
+            with nc.allow_non_contiguous_dma(reason="one value a partition"):
                 if i < 2:
+                    half_q = slice(i * HALF_P // RUN, (i + 1) * HALF_P // RUN)
                     for t in range(2):
-                        nc.sync.dma_start(
-                            out=gain[i][64 * t : 64 * t + 64, :], in_=unit_rows[t, 16 * i : 16 * i + 16]
-                        )
+                        nc.sync.dma_start(out=gain[i][t * HALF_P : (t + 1) * HALF_P, :], in_=unit_rows[t, half_q])
                 else:
                     nc.sync.dma_start(out=gain[i][:], in_=unit_rows[i])
 
-        load_w1(0)
-        nc.sync.dma_start(lists[0][:], offs)
         for g in range(PASSES):
-            nc.sync.dma_start(
-                out=table[g][:].bitcast(I32), in_=x_words[g].rearrange("p n r -> p (n r)").bitcast(I32)
-            )
+            load_w1(0, g)
+        nc.sync.dma_start(pick_list[:], offs)
+        for g in range(PASSES):
+            words = x_words[g].rearrange("p n r -> p (n r)")
+            nc.sync.dma_start(out=table[g][:].bitcast(I32), in_=words.bitcast(I32))
+        load_w1(1, 0)
         load_gain(0)
-        for dst, src in zip(lists[1:], (p1, p2, p3)):
+        load_w1(1, 1)
+        for dst, src in zip(partner_lists, (p1, p2, p3)):
             nc.sync.dma_start(dst[:], src)
-        load_w1(1)
         for i in range(1, PACK):
             load_gain(i)
         for t in range(PACK):
             nc.sync.dma_start(out=w2_raw[:, t, :], in_=w2_rows[t])
 
-        for quad in range(4):
-            rows = slice(32 * quad, 32 * quad + 4 * PASSES)
+        for rows in live_rows:
             nc.vector.tensor_copy(table_scales[rows, :].bitcast(I32), scale_rows[rows, :])
 
-        w1_bf = [tiles(f"w1_bf{h}_", PASSES, [P, PACK * H // 2], BF16) for h in range(2)]
-        early_codes = [tiles(f"early_codes{h}_", PASSES, [P, P], U32) for h in range(2)]
-        early_scales = [tiles(f"early_scales{h}_", PASSES, [P, P], U8) for h in range(2)]
-        late_codes = tiles("late_codes", PASSES, [P, 2 * P], U32)
-        late_scales = tiles("late_scales", PASSES, [P, 2 * P], U8)
+        w1_bf = [tiles(f"w1_bf{h}_", PASSES, [P, PACK * HALF_H], BF16) for h in range(2)]
+        w1_codes = [tiles(f"w1_codes{i}_", PASSES, [P, P], U32) for i in range(PACK)]
+        w1_scales = [tiles(f"w1_scales{i}_", PASSES, [P, P], U8) for i in range(PACK)]
+        byte_width = PACK * HALF_P
 
         def round_w1(copy, h, g):
             copy(
-                out=w1_bf[h][g][:].rearrange("p (t q c j) -> p q t j c", t=PACK, c=4, j=PACK),
-                in_=w1_raw[h][g][:].rearrange("p j (q t c) -> p q t j c", t=PACK, c=4),
+                out=w1_bf[h][g][:].rearrange("p (t q c j) -> p q t j c", t=PACK, c=RUN, j=PACK),
+                in_=w1_raw[h][g][:].rearrange("p j (q t c) -> p q t j c", t=PACK, c=RUN),
             )
 
-        def quantise_early(h, g):
-            quantise(early_codes[h][g], early_scales[h][g], w1_bf[h][g][:, : 2 * 256])
+        def quantise_own_tile(h, g):
+            quantise(w1_codes[h][g][:], w1_scales[h][g][:], w1_bf[h][g][:, : 2 * byte_width])
 
-        def quantise_late(h, g):
+        def quantise_shared_tiles(h, g):
+            cols = slice(h * HALF_P, (h + 1) * HALF_P)
             for t in (2, 3):
-                cols = slice((t - 2) * P + 64 * h, (t - 2) * P + 64 * h + 64)
-                quantise(late_codes[g][:, cols], late_scales[g][:, cols], w1_bf[h][g][:, 256 * t : 256 * t + 256])
+                values = w1_bf[h][g][:, t * byte_width : (t + 1) * byte_width]
+                quantise(w1_codes[t][g][:, cols], w1_scales[t][g][:, cols], values)
 
-        def quantise(codes, scales, values):
-            nc.vector.quantize_mx(out=codes[:].bitcast(FP8X4), scales=scales[:], in_=values)
+        round_w1(nc.vector.tensor_copy, 0, 0)
+        round_w1(nc.scalar.copy, 0, 1)
+        for g in range(PASSES):
+            quantise_own_tile(0, g)
+            quantise_shared_tiles(0, g)
 
-        picked_scales = sb.tile([P, S], U8, align_bytes=64)
-        y = [ps.tile([P, S], F32, name=f"y{t}") for t in range(PACK)]
+        picked_scales = tile("picked_scales", [P, S], U8)
+        nc.vector.tensor_copy(picked_scales[:], table_scales[:].indirect(pick_list[:]))
+        picked = [tile("picked0", [P, S], U32, tag="table_scales"), tile("picked1", [P, S], U32)]
+        y = [ps.tile([P, S], F32, name=f"y{i}") for i in range(PACK)]
 
-        def product(i, g):
-            if i < 2:
-                codes, scales = early_codes[i][g][:], early_scales[i][g][:]
-            else:
-                cols = slice((i - 2) * P, (i - 1) * P)
-                codes, scales = late_codes[g][:, cols], late_scales[g][:, cols]
+        def first_product(i, g):
             nc.tensor.matmul_mx(
                 out=y[i][:],
-                lhsT=codes.bitcast(FP8X4),
-                lhsT_scale=scales,
+                lhsT=w1_codes[i][g][:].bitcast(FP8X4),
+                lhsT_scale=w1_scales[i][g][:],
                 rhs=picked[g][:].bitcast(FP8X4),
-                rhs_scale=picked_scales[4 * g :, :],
+                rhs_scale=picked_scales[SCALE_ROWS * g :, :],
                 start=(g == 0),
                 stop=(g == PASSES - 1),
             )
 
         for g in range(PASSES):
-            round_w1(nc.vector.tensor_copy, 0, g)
-        for g in range(PASSES):
-            quantise_early(0, g)
-            quantise_late(0, g)
-        nc.vector.tensor_copy(picked_scales[:], table_scales[:].indirect(lists[0][:]))
-        picked = [
-            sb.tile([P, S], U32, name="picked0", align_bytes=64, tag="shared"),
-            sb.tile([P, S], U32, name="picked1", align_bytes=64),
-        ]
-        for g in range(PASSES):
-            nc.vector.tensor_copy(picked[g][:], table[g][:].indirect(lists[0][:]))
-            product(0, g)
-
-        w2_bf = sb.tile([P, N * PACK], BF16, align_bytes=64)
-        w2_codes = sb.tile([P, N], U32, align_bytes=64)
-        w2_scales = sb.tile([P, N], U8, align_bytes=64)
-
-        def prepare_w2():
-            nc.vector.tensor_copy(
-                out=w2_bf[:].rearrange("p (a c t) -> p a t c", c=4, t=PACK),
-                in_=w2_raw[:].rearrange("p t (a c) -> p a t c", c=4),
-            )
-
-        def quantise_w2():
-            nc.vector.quantize_mx(out=w2_codes[:].bitcast(FP8X4), scales=w2_scales[:], in_=w2_bf[:])
+            nc.vector.tensor_copy(picked[g][:], table[g][:].indirect(pick_list[:]))
+            first_product(0, g)
 
         squares = tiles("squares", PACK, [P, S], BF16)
         total = tiles("total", PACK, [P, 1], F32)
-        stats = sb.tile([P, 6], F32)
-        moments = sb.tile([P, 2], F32)
-        staged = sb.tile([P, S], F32, align_bytes=64)
         rstd = tiles("rstd", PACK, [P, 1], F32)
-        a1 = tiles("a1_", PACK, [P, S], F32)
-        a2 = tiles("a2_", PACK, [P, S], F32)
-        a3 = tiles("a3_", PACK, [P, S], F32)
-        low = tiles("low", PACK, [P, S], F32)
+        factor = tiles("factor", PACK, [P, 1], F32)
+        partner = [
+            [tile(f"partner{i}_{k}", [P, S], F32, tag="w1_bf1_1" if (i, k) == (0, 1) else None) for k in range(3)]
+            for i in range(PACK)
+        ]
+        capped = [tile(f"capped{i}", [P, S], F32, tag=f"high{i + 1}") for i in range(PACK)]
+        median = [tile(f"median{i}", [P, S], F32, tag=f"low{i + 1}") for i in range(PACK)]
         high = tiles("high", PACK, [P, S], F32)
-        capped = tiles("capped", PACK, [P, S], F32)
-        median = tiles("median", PACK, [P, S], F32)
-        hid = sb.tile([P, PACK, S], F32, align_bytes=64)
-        halves = [slice(0, HALF), slice(HALF, S)]
-        whole = slice(0, S)
+        low = tiles("low", PACK, [P, S], F32)
+        hid = tile("hid", [P, PACK, S], F32)
+        staged = tile("staged", [P, S], F32)
+        halves = [slice(0, HALF_S), slice(HALF_S, S)]
 
-        def sum_squares(t):
-            nc.scalar.activation(out=squares[t][:], in_=y[t][:], func=ACT.Square, accum_out=total[t][:])
-
-        def take_root(t, scale):
+        def norm(i):
+            nc.scalar.activation(out=squares[i][:], in_=y[i][:], func=ACT.Square, accum_out=total[i][:])
             nc.scalar.activation(
-                out=rstd[t][:], in_=total[t][:], func=ACT.Abs_reciprocal_sqrt, scale=scale, bias=EPS
+                out=rstd[i][:], in_=total[i][:], func=ACT.Abs_reciprocal_sqrt, scale=1.0 / S, bias=EPS
             )
 
-        def scale_out(t):
-            nc.vector.tensor_scalar(z[t][:, :S], y[t][:], rstd[t][:], gain[t][:], ALU.mult, ALU.mult)
+        def scale_out_on_vector(i):
+            nc.vector.tensor_scalar(z[i][:, :S], y[i][:], rstd[i][:], gain[i][:], ALU.mult, ALU.mult)
 
-        def partners(t, which, cols):
-            return z[t][:].indirect(lists[which][:, cols.start // LIST_ROWS : cols.stop // LIST_ROWS])
+        def scale_out_on_scalar(i):
+            nc.scalar.activation(out=factor[i][:], in_=rstd[i][:], func=ACT.Copy, scale=gain[i][:])
+            nc.scalar.activation(out=z[i][:, :S], in_=y[i][:], func=ACT.Copy, scale=factor[i][:])
 
-        def fetch_scalar(dst, t, which, cols):
-            nc.scalar.activation(out=dst[t][:, cols], in_=partners(t, which, cols), func=ACT.Copy)
+        def fetch_partners(i):
+            for k in range(3):
+                picks = z[i][:].indirect(partner_lists[k][:])
+                if k == 1 and i < PACK - 1:
+                    nc.vector.tensor_copy(partner[i][k][:], picks)
+                else:
+                    nc.scalar.activation(out=partner[i][k][:], in_=picks, func=ACT.Copy)
 
-        def order_two(t, cols):
-            nc.vector.tensor_tensor(high[t][:, cols], a1[t][:, cols], a2[t][:, cols], ALU.max)
-            nc.vector.tensor_tensor(low[t][:, cols], a1[t][:, cols], a2[t][:, cols], ALU.min)
-
-        def cap(t, c):
-            nc.vector.tensor_tensor(capped[t][:, c], high[t][:, c], a3[t][:, c], ALU.min)
-
-        def lift(t, c):
-            nc.vector.tensor_tensor(median[t][:, c], capped[t][:, c], low[t][:, c], ALU.max)
-
-        def mix(t, c):
-            dst = staged[:, c] if t == 1 else hid[:, t, c]
-            nc.vector.scalar_tensor_tensor(dst, z[t][:, c], 0.5, median[t][:, c], ALU.mult, ALU.add)
-
-        def finish(t, cols):
-            mid = (cols.start + cols.stop) // 2
-            for step in (cap, lift, mix):
-                step(t, slice(cols.start, mid))
-                step(t, slice(mid, cols.stop))
+        def mix(i):
+            first, second, third = partner[i]
+            nc.vector.tensor_tensor(high[i][:], first[:], second[:], ALU.max)
+            nc.vector.tensor_tensor(low[i][:], first[:], second[:], ALU.min)
+            for c in halves:
+                nc.vector.tensor_tensor(capped[i][:, c], high[i][:, c], third[:, c], ALU.min)
+            for c in halves:
+                nc.vector.tensor_tensor(median[i][:, c], capped[i][:, c], low[i][:, c], ALU.max)
+            for c in halves:
+                dst = staged[:, c] if i == 1 else hid[:, i, c]
+                nc.vector.scalar_tensor_tensor(dst, z[i][:, c], 0.5, median[i][:, c], ALU.mult, ALU.add)
 
         round_w1(nc.vector.tensor_copy, 1, 0)
-        nc.vector.bn_stats(stats[:], y[0][:])
-        quantise_early(1, 0)
-        product(1, 0)
-        nc.vector.bn_aggr(moments[:], stats[:])
-        nc.vector.scalar_tensor_tensor(
-            total[0][:], moments[:, 0:1], moments[:, 0:1], moments[:, 1:2], ALU.mult, ALU.add
-        )
-        take_root(0, 1.0)
-        quantise_late(1, 0)
-        scale_out(0)
-        round_w1(nc.scalar.copy, 1, 1)
-        fetch_scalar(a1, 0, 1, whole)
-        quantise_early(1, 1)
-        product(1, 1)
-        quantise_late(1, 1)
+        norm(0)
+        quantise_own_tile(1, 0)
+        first_product(1, 0)
+        quantise_shared_tiles(1, 0)
+        round_w1(nc.vector.tensor_copy, 1, 1)
+        scale_out_on_vector(0)
+        quantise_own_tile(1, 1)
+        first_product(1, 1)
+        quantise_shared_tiles(1, 1)
         for i in (2, 3):
             for g in range(PASSES):
-                product(i, g)
-        nc.vector.tensor_copy(a2[0][:], partners(0, 2, whole))
-        sum_squares(1)
-        take_root(1, 1.0 / S)
-        fetch_scalar(a3, 0, 3, whole)
-        scale_out(1)
-        order_two(0, whole)
-        finish(0, whole)
-        nc.sync.dma_start(out=hid[0:64, 1, :], in_=hid[64:128, 0, :])
-        fetch_scalar(a1, 1, 1, whole)
-        fetch_scalar(a2, 1, 2, whole)
-        sum_squares(2)
-        take_root(2, 1.0 / S)
-        fetch_scalar(a3, 1, 3, whole)
-        order_two(1, whole)
-        scale_out(2)
-        cap(1, whole)
-        prepare_w2()
-        lift(1, whole)
-        quantise_w2()
-        mix(1, whole)
-        nc.sync.dma_start(out=hid[64:128, 0, :], in_=staged[0:64, :])
-        nc.sync.dma_start(out=hid[64:128, 1, :], in_=staged[64:128, :])
-        fetch_scalar(a1, 2, 1, whole)
-        sum_squares(3)
-        take_root(3, 1.0 / S)
-        fetch_scalar(a2, 2, 2, whole)
-        fetch_scalar(a3, 2, 3, whole)
-        scale_out(3)
-        order_two(2, whole)
-        finish(2, whole)
-        last = PACK - 1
-        for cols in halves:
-            fetch_scalar(a1, last, 1, cols)
-            fetch_scalar(a2, last, 2, cols)
-            fetch_scalar(a3, last, 3, cols)
-            order_two(last, cols)
-            finish(last, cols)
+                first_product(i, g)
 
-        hid_bf = tiles("hid_bf", 2, [P, HALF * PACK], BF16)
-        hid_codes = tiles("hid_codes", 2, [P, HALF], U32)
-        hid_scales = tiles("hid_scales", 2, [P, HALF], U8)
-        result = tiles("result", 2, [P, HALF], F32)
-        acc = [ps.tile([P, HALF], F32, name=f"acc{i}") for i in range(2)]
-        movers = (nc.scalar.copy, nc.vector.tensor_copy)
+        w2_bf = tile("w2_bf", [P, N * PACK], BF16)
+        w2_codes = tile("w2_codes", [P, N], U32)
+        w2_scales = tile("w2_scales", [P, N], U8)
+        lower, upper = slice(0, HALF_P), slice(HALF_P, P)
 
-        def interleave(copy, i, first, count):
+        fetch_partners(0)
+        for i in range(1, PACK):
+            norm(i)
+        scale_out_on_scalar(1)
+        scale_out_on_scalar(2)
+        mix(0)
+        nc.sync.dma_start(out=hid[lower, 1, :], in_=hid[upper, 0, :])
+        nc.vector.tensor_copy(
+            out=w2_bf[:].rearrange("p (a c t) -> p a t c", c=RUN, t=PACK),
+            in_=w2_raw[:].rearrange("p t (a c) -> p a t c", c=RUN),
+        )
+        fetch_partners(1)
+        scale_out_on_scalar(3)
+        mix(1)
+        nc.sync.dma_start(out=hid[upper, 0, :], in_=staged[lower, :])
+        nc.sync.dma_start(out=hid[upper, 1, :], in_=staged[upper, :])
+        quantise(w2_codes[:], w2_scales[:], w2_bf[:])
+        for i in (2, 3):
+            fetch_partners(i)
+            mix(i)
+
+        hid_bf = tiles("hid_bf", 2, [P, HALF_S * PACK], BF16)
+        hid_codes = tiles("hid_codes", 2, [P, HALF_S], U32)
+        hid_scales = tiles("hid_scales", 2, [P, HALF_S], U8)
+        result = tiles("result", 2, [P, HALF_S], F32)
+        acc = [ps.tile([P, HALF_S], F32, name=f"acc{u}") for u in range(2)]
+
+        def interleave(copy, u, start, stop):
             copy(
-                out=hid_bf[i][:, PACK * first : PACK * (first + count)].rearrange("p (a c t) -> p a t c", c=4, t=PACK),
-                in_=hid[:, :, i * HALF + first : i * HALF + first + count].rearrange("p t (a c) -> p a t c", c=4),
+                out=hid_bf[u][:, PACK * start : PACK * stop].rearrange("p (a c t) -> p a t c", c=RUN, t=PACK),
+                in_=hid[:, :, u * HALF_S + start : u * HALF_S + stop].rearrange("p t (a c) -> p a t c", c=RUN),
             )
 
-        interleave(nc.scalar.copy, 0, 0, HALF)
-        interleave(nc.vector.tensor_copy, 1, 0, 160)
-        interleave(nc.scalar.copy, 1, 160, HALF - 160)
-        for i, cols in enumerate(halves):
-            nc.vector.quantize_mx(out=hid_codes[i][:].bitcast(FP8X4), scales=hid_scales[i][:], in_=hid_bf[i][:])
+        interleave(nc.scalar.copy, 0, 0, SCALAR_TOKENS)
+        interleave(nc.vector.tensor_copy, 1, 0, HALF_S)
+        interleave(nc.vector.tensor_copy, 0, SCALAR_TOKENS, HALF_S)
+        for u in (1, 0):
+            quantise(hid_codes[u][:], hid_scales[u][:], hid_bf[u][:])
             nc.tensor.matmul_mx(
-                out=acc[i][:],
+                out=acc[u][:],
                 lhsT=w2_codes[:].bitcast(FP8X4),
                 lhsT_scale=w2_scales[:],
-                rhs=hid_codes[i][:].bitcast(FP8X4),
-                rhs_scale=hid_scales[i][:],
+                rhs=hid_codes[u][:].bitcast(FP8X4),
+                rhs_scale=hid_scales[u][:],
                 start=True,
                 stop=True,
             )
-        for i, cols in enumerate(halves):
-            movers[i](out=result[i][:], in_=acc[i][:])
-            nc.sync.dma_start(out=out[:, cols], in_=result[i][:])
+        for u, copy in ((1, nc.scalar.copy), (0, nc.vector.tensor_copy)):
+            copy(out=result[u][:], in_=acc[u][:])
+            nc.sync.dma_start(out=out[:, halves[u]], in_=result[u][:])

@@ -21,6 +21,7 @@ RUN = 4
 K_PASS = P * PACK
 PASSES = K // K_PASS
 QUADRANT = 32
+QUADRANTS = P // QUADRANT
 SCALE_ROWS = 4
 LIST_ROWS = 16
 HALF_P = P // 2
@@ -58,10 +59,10 @@ def tile_picked_ygossip_med_p_kernel(
         w2_raw = tile("w2_raw", [P, PACK, N], F32)
         z = tiles("z", PACK, [P, WINDOW], F32)
 
-        live_rows = [slice(QUADRANT * quad, QUADRANT * quad + SCALE_ROWS * PASSES) for quad in range(4)]
-        for quad, queue in enumerate((nc.sync, nc.sync, nc.sync, nc.sync)):
+        live_rows = [slice(QUADRANT * quad, QUADRANT * quad + SCALE_ROWS * PASSES) for quad in range(QUADRANTS)]
+        for quad in range(QUADRANTS):
             rows = x_scales[:, SCALE_ROWS * quad : SCALE_ROWS * (quad + 1), :]
-            queue.dma_start(out=scale_rows[live_rows[quad], :], in_=rows.bitcast(I32))
+            nc.sync.dma_start(out=scale_rows[live_rows[quad], :], in_=rows.bitcast(I32))
         nc.vector.memset(table_scales[:].bitcast(I32), 0)
         for t in range(PACK):
             nc.vector.memset(z[t][:, S:], 0.0)
@@ -85,6 +86,7 @@ def tile_picked_ygossip_med_p_kernel(
                 else:
                     nc.sync.dma_start(out=gain[i][:], in_=unit_rows[i])
 
+        norm_order = (1, 2, 0, 3)
         for g in range(PASSES):
             load_w1(0, g)
         nc.sync.dma_start(pick_list[:], offs)
@@ -92,11 +94,10 @@ def tile_picked_ygossip_med_p_kernel(
             words = x_words[g].rearrange("p n r -> p (n r)")
             nc.sync.dma_start(out=table[g][:].bitcast(I32), in_=words.bitcast(I32))
         load_w1(1, 0)
-        load_gain(0)
-        load_w1(1, 1)
         for dst, src in zip(partner_lists, (p1, p2, p3)):
             nc.sync.dma_start(dst[:], src)
-        for i in range(1, PACK):
+        load_w1(1, 1)
+        for i in norm_order:
             load_gain(i)
         for t in range(PACK):
             nc.sync.dma_start(out=w2_raw[:, t, :], in_=w2_rows[t])
@@ -135,25 +136,28 @@ def tile_picked_ygossip_med_p_kernel(
         picked = [tile("picked0", [P, S], U32, tag="table_scales"), tile("picked1", [P, S], U32)]
         y = [ps.tile([P, S], F32, name=f"y{i}") for i in range(PACK)]
 
-        def first_product(i, g):
+        def first_product(i, g, cols=slice(0, S)):
             nc.tensor.matmul_mx(
-                out=y[i][:],
+                out=y[i][:, cols],
                 lhsT=w1_codes[i][g][:].bitcast(FP8X4),
                 lhsT_scale=w1_scales[i][g][:],
-                rhs=picked[g][:].bitcast(FP8X4),
-                rhs_scale=picked_scales[SCALE_ROWS * g :, :],
+                rhs=picked[g][:, cols].bitcast(FP8X4),
+                rhs_scale=picked_scales[SCALE_ROWS * g :, cols],
                 start=(g == 0),
-                stop=(g == PASSES - 1),
+                stop=(g == PASSES - 1 and cols.stop == S),
             )
 
-        for g in range(PASSES):
-            nc.vector.tensor_copy(picked[g][:], table[g][:].indirect(pick_list[:]))
-            first_product(0, g)
+        nc.vector.tensor_copy(picked[0][:], table[0][:].indirect(pick_list[:]))
+        first_product(0, 0)
+        for cols in (slice(0, HALF_S), slice(HALF_S, S)):
+            entries = pick_list[:, cols.start // LIST_ROWS : cols.stop // LIST_ROWS]
+            nc.vector.tensor_copy(picked[1][:, cols], table[1][:].indirect(entries))
+            first_product(0, 1, cols)
 
         squares = tiles("squares", PACK, [P, S], BF16)
         total = tiles("total", PACK, [P, 1], F32)
         rstd = tiles("rstd", PACK, [P, 1], F32)
-        factor = tiles("factor", PACK, [P, 1], F32)
+        factor = {i: tile(f"factor{i}", [P, 1], F32) for i in range(1, PACK)}
         partner = [
             [tile(f"partner{i}_{k}", [P, S], F32, tag="w1_bf1_1" if (i, k) == (0, 1) else None) for k in range(3)]
             for i in range(PACK)
@@ -163,7 +167,7 @@ def tile_picked_ygossip_med_p_kernel(
         high = tiles("high", PACK, [P, S], F32)
         low = tiles("low", PACK, [P, S], F32)
         hid = tile("hid", [P, PACK, S], F32)
-        staged = tile("staged", [P, S], F32)
+        staged = tiles("staged", 2, [P, S], F32)
         halves = [slice(0, HALF_S), slice(HALF_S, S)]
 
         def norm(i):
@@ -172,10 +176,7 @@ def tile_picked_ygossip_med_p_kernel(
                 out=rstd[i][:], in_=total[i][:], func=ACT.Abs_reciprocal_sqrt, scale=1.0 / S, bias=EPS
             )
 
-        def scale_out_on_vector(i):
-            nc.vector.tensor_scalar(z[i][:, :S], y[i][:], rstd[i][:], gain[i][:], ALU.mult, ALU.mult)
-
-        def scale_out_on_scalar(i):
+        def scale_out(i):
             nc.scalar.activation(out=factor[i][:], in_=rstd[i][:], func=ACT.Copy, scale=gain[i][:])
             nc.scalar.activation(out=z[i][:, :S], in_=y[i][:], func=ACT.Copy, scale=factor[i][:])
 
@@ -196,16 +197,15 @@ def tile_picked_ygossip_med_p_kernel(
             for c in halves:
                 nc.vector.tensor_tensor(median[i][:, c], capped[i][:, c], low[i][:, c], ALU.max)
             for c in halves:
-                dst = staged[:, c] if i == 1 else hid[:, i, c]
+                dst = staged[i][:, c] if i < 2 else hid[:, i, c]
                 nc.vector.scalar_tensor_tensor(dst, z[i][:, c], 0.5, median[i][:, c], ALU.mult, ALU.add)
 
         round_w1(nc.vector.tensor_copy, 1, 0)
-        norm(0)
+        nc.scalar.copy(out=z[0][:, :S], in_=y[0][:])
         quantise_own_tile(1, 0)
         first_product(1, 0)
         quantise_shared_tiles(1, 0)
         round_w1(nc.vector.tensor_copy, 1, 1)
-        scale_out_on_vector(0)
         quantise_own_tile(1, 1)
         first_product(1, 1)
         quantise_shared_tiles(1, 1)
@@ -219,21 +219,22 @@ def tile_picked_ygossip_med_p_kernel(
         lower, upper = slice(0, HALF_P), slice(HALF_P, P)
 
         fetch_partners(0)
-        for i in range(1, PACK):
+        for i in norm_order:
             norm(i)
-        scale_out_on_scalar(1)
-        scale_out_on_scalar(2)
+        scale_out(1)
+        scale_out(2)
         mix(0)
+        nc.vector.tensor_scalar(hid[:, 0, :], staged[0][:], rstd[0][:], gain[0][:], ALU.mult, ALU.mult)
         nc.sync.dma_start(out=hid[lower, 1, :], in_=hid[upper, 0, :])
         nc.vector.tensor_copy(
             out=w2_bf[:].rearrange("p (a c t) -> p a t c", c=RUN, t=PACK),
             in_=w2_raw[:].rearrange("p t (a c) -> p a t c", c=RUN),
         )
         fetch_partners(1)
-        scale_out_on_scalar(3)
+        scale_out(3)
         mix(1)
-        nc.sync.dma_start(out=hid[upper, 0, :], in_=staged[lower, :])
-        nc.sync.dma_start(out=hid[upper, 1, :], in_=staged[upper, :])
+        nc.sync.dma_start(out=hid[upper, 0, :], in_=staged[1][lower, :])
+        nc.sync.dma_start(out=hid[upper, 1, :], in_=staged[1][upper, :])
         quantise(w2_codes[:], w2_scales[:], w2_bf[:])
         for i in (2, 3):
             fetch_partners(i)

from contextlib import ExitStack

import concourse.mybir as mybir

K, T, S, N, H = 1024, 2048, 512, 128, 512
FLOPS = 2 * K * H * S + 2 * H * N * S

F32 = mybir.dt.float32
BF16 = mybir.dt.bfloat16
I32 = mybir.dt.int32
U32 = mybir.dt.uint32
U16 = mybir.dt.uint16
U8 = mybir.dt.uint8
FP8X4 = mybir.dt.float8_e4m3fn_x4
ALU = mybir.AluOpType
ACT = mybir.ActivationFunctionType

P = 128
PACK = 4
RUN = 4
K_PASS = P * PACK
PASSES = K // K_PASS
QUADRANT = 32
QUADRANTS = P // QUADRANT
SCALE_ROWS = 4
LIST_ROWS = 16
HALF_P = P // 2
HALF_H = H // 2
HALF_S = S // 2
WINDOW = 704
SCALAR_TOKENS = 192
EPS = 0.1


def tile_picked_ygossip_med_p_kernel(
    tc, x_words, x_scales, w1, unit, w2, offs, p1, p2, p3, out
):
    nc = tc.nc
    with ExitStack() as ctx:
        sb = ctx.enter_context(tc.tile_pool(name="sb", bufs=1))
        ps = ctx.enter_context(tc.psum_pool(name="ps", bufs=1))

        def tile(name, shape, dtype, tag=None):
            return sb.tile(shape, dtype, name=name, tag=tag or name, align_bytes=64)

        def tiles(name, count, shape, dtype):
            return [tile(f"{name}{i}", shape, dtype) for i in range(count)]

        def quantise(codes, scales, values):
            nc.vector.quantize_mx(out=codes.bitcast(FP8X4), scales=scales, in_=values)

        pick_list = tile("pick_list", [P, S // LIST_ROWS], U16)
        partner_lists = tiles("partner_list", 3, [P, S // LIST_ROWS], U16)
        w1_raw = [tiles(f"w1_raw{h}_", PASSES, [P, PACK, HALF_H], F32) for h in range(2)]
        table = tiles("table", PASSES, [P, T], U32)
        scale_rows = tile("scale_rows", [P, T // 4], I32)
        table_scales = tile("table_scales", [P, T], U8)
        gain = tiles("gain", PACK, [P, 1], F32)
        w2_raw = tile("w2_raw", [P, PACK, N], F32)
        z = tiles("z", PACK, [P, WINDOW], F32)

        live_rows = [slice(QUADRANT * quad, QUADRANT * quad + SCALE_ROWS * PASSES) for quad in range(QUADRANTS)]
        for quad in range(QUADRANTS):
            rows = x_scales[:, SCALE_ROWS * quad : SCALE_ROWS * (quad + 1), :]
            nc.sync.dma_start(out=scale_rows[live_rows[quad], :], in_=rows.bitcast(I32))
        nc.vector.memset(table_scales[:].bitcast(I32), 0)
        for t in range(PACK):
            nc.vector.memset(z[t][:, S:], 0.0)

        warm_up = tile("warm_up", [P, 1], F32)
        nc.scalar.activation(out=warm_up[:], in_=z[0][:, S : S + 1], func=ACT.Abs_reciprocal_sqrt, bias=EPS)

        w2_rows = w2.rearrange("(q t c) n -> t q c n", t=PACK, c=RUN)
        unit_rows = unit.rearrange("(q t c) o -> t q c o", t=PACK, c=RUN)

        def load_w1(h, g):
            rows = w1[g * K_PASS : (g + 1) * K_PASS, h * HALF_H : (h + 1) * HALF_H]
            nc.sync.dma_start(out=w1_raw[h][g][:], in_=rows.rearrange("(p j) n -> p j n", j=PACK))

        def load_gain(i):
            with nc.allow_non_contiguous_dma(reason="one value a partition"):
                if i < 2:
                    half_q = slice(i * HALF_P // RUN, (i + 1) * HALF_P // RUN)
                    for t in range(2):
                        nc.sync.dma_start(out=gain[i][t * HALF_P : (t + 1) * HALF_P, :], in_=unit_rows[t, half_q])
                else:
                    nc.sync.dma_start(out=gain[i][:], in_=unit_rows[i])

        norm_order = (1, 2, 0, 3)
        for g in range(PASSES):
            load_w1(0, g)
        nc.sync.dma_start(pick_list[:], offs)
        for g in range(PASSES):
            words = x_words[g].rearrange("p n r -> p (n r)")
            nc.sync.dma_start(out=table[g][:].bitcast(I32), in_=words.bitcast(I32))
        load_w1(1, 0)
        for dst, src in zip(partner_lists, (p1, p2, p3)):
            nc.sync.dma_start(dst[:], src)
        load_w1(1, 1)
        for i in norm_order:
            load_gain(i)
        for t in range(PACK):
            nc.sync.dma_start(out=w2_raw[:, t, :], in_=w2_rows[t])

        for rows in live_rows:
            nc.vector.tensor_copy(table_scales[rows, :].bitcast(I32), scale_rows[rows, :])

        w1_bf = [tiles(f"w1_bf{h}_", PASSES, [P, PACK * HALF_H], BF16) for h in range(2)]
        w1_codes = [tiles(f"w1_codes{i}_", PASSES, [P, P], U32) for i in range(PACK)]
        w1_scales = [tiles(f"w1_scales{i}_", PASSES, [P, P], U8) for i in range(PACK)]
        byte_width = PACK * HALF_P

        def round_w1(copy, h, g):
            copy(
                out=w1_bf[h][g][:].rearrange("p (t q c j) -> p q t j c", t=PACK, c=RUN, j=PACK),
                in_=w1_raw[h][g][:].rearrange("p j (q t c) -> p q t j c", t=PACK, c=RUN),
            )

        def quantise_own_tile(h, g):
            quantise(w1_codes[h][g][:], w1_scales[h][g][:], w1_bf[h][g][:, : 2 * byte_width])

        def quantise_shared_tiles(h, g):
            cols = slice(h * HALF_P, (h + 1) * HALF_P)
            for t in (2, 3):
                values = w1_bf[h][g][:, t * byte_width : (t + 1) * byte_width]
                quantise(w1_codes[t][g][:, cols], w1_scales[t][g][:, cols], values)

        round_w1(nc.vector.tensor_copy, 0, 0)
        round_w1(nc.scalar.copy, 0, 1)
        for g in range(PASSES):
            quantise_own_tile(0, g)
            quantise_shared_tiles(0, g)

        picked_scales = tile("picked_scales", [P, S], U8)
        nc.vector.tensor_copy(picked_scales[:], table_scales[:].indirect(pick_list[:]))
        picked = [tile("picked0", [P, S], U32, tag="table_scales"), tile("picked1", [P, S], U32)]
        y = [ps.tile([P, S], F32, name=f"y{i}") for i in range(PACK)]

        def first_product(i, g, cols=slice(0, S)):
            nc.tensor.matmul_mx(
                out=y[i][:, cols],
                lhsT=w1_codes[i][g][:].bitcast(FP8X4),
                lhsT_scale=w1_scales[i][g][:],
                rhs=picked[g][:, cols].bitcast(FP8X4),
                rhs_scale=picked_scales[SCALE_ROWS * g :, cols],
                start=(g == 0),
                stop=(g == PASSES - 1 and cols.stop == S),
            )

        nc.vector.tensor_copy(picked[0][:], table[0][:].indirect(pick_list[:]))
        first_product(0, 0)
        for cols in (slice(0, HALF_S), slice(HALF_S, S)):
            entries = pick_list[:, cols.start // LIST_ROWS : cols.stop // LIST_ROWS]
            nc.vector.tensor_copy(picked[1][:, cols], table[1][:].indirect(entries))
            first_product(0, 1, cols)

        squares = tiles("squares", PACK, [P, S], BF16)
        total = tiles("total", PACK, [P, 1], F32)
        rstd = tiles("rstd", PACK, [P, 1], F32)
        factor = {i: tile(f"factor{i}", [P, 1], F32) for i in range(1, PACK)}
        partner = [
            [tile(f"partner{i}_{k}", [P, S], F32, tag="w1_bf1_1" if (i, k) == (0, 1) else None) for k in range(3)]
            for i in range(PACK)
        ]
        capped = [tile(f"capped{i}", [P, S], F32, tag=f"high{i + 1}") for i in range(PACK)]
        median = [tile(f"median{i}", [P, S], F32, tag=f"low{i + 1}") for i in range(PACK)]
        high = tiles("high", PACK, [P, S], F32)
        low = tiles("low", PACK, [P, S], F32)
        hid = tile("hid", [P, PACK, S], F32)
        staged = tiles("staged", 2, [P, S], F32)
        halves = [slice(0, HALF_S), slice(HALF_S, S)]

        def norm(i):
            nc.scalar.activation(out=squares[i][:], in_=y[i][:], func=ACT.Square, accum_out=total[i][:])
            nc.scalar.activation(
                out=rstd[i][:], in_=total[i][:], func=ACT.Abs_reciprocal_sqrt, scale=1.0 / S, bias=EPS
            )

        def scale_out(i):
            nc.scalar.activation(out=factor[i][:], in_=rstd[i][:], func=ACT.Copy, scale=gain[i][:])
            nc.scalar.activation(out=z[i][:, :S], in_=y[i][:], func=ACT.Copy, scale=factor[i][:])

        def fetch_partners(i):
            for k in range(3):
                picks = z[i][:].indirect(partner_lists[k][:])
                if k == 1 and i < PACK - 1:
                    nc.vector.tensor_copy(partner[i][k][:], picks)
                else:
                    nc.scalar.activation(out=partner[i][k][:], in_=picks, func=ACT.Copy)

        def mix(i):
            first, second, third = partner[i]
            nc.vector.tensor_tensor(high[i][:], first[:], second[:], ALU.max)
            nc.vector.tensor_tensor(low[i][:], first[:], second[:], ALU.min)
            for c in halves:
                nc.vector.tensor_tensor(capped[i][:, c], high[i][:, c], third[:, c], ALU.min)
            for c in halves:
                nc.vector.tensor_tensor(median[i][:, c], capped[i][:, c], low[i][:, c], ALU.max)
            for c in halves:
                dst = staged[i][:, c] if i < 2 else hid[:, i, c]
                nc.vector.scalar_tensor_tensor(dst, z[i][:, c], 0.5, median[i][:, c], ALU.mult, ALU.add)

        round_w1(nc.vector.tensor_copy, 1, 0)
        nc.scalar.copy(out=z[0][:, :S], in_=y[0][:])
        quantise_own_tile(1, 0)
        first_product(1, 0)
        quantise_shared_tiles(1, 0)
        round_w1(nc.vector.tensor_copy, 1, 1)
        quantise_own_tile(1, 1)
        first_product(1, 1)
        quantise_shared_tiles(1, 1)
        for i in (2, 3):
            for g in range(PASSES):
                first_product(i, g)

        w2_bf = tile("w2_bf", [P, N * PACK], BF16)
        w2_codes = tile("w2_codes", [P, N], U32)
        w2_scales = tile("w2_scales", [P, N], U8)
        lower, upper = slice(0, HALF_P), slice(HALF_P, P)

        fetch_partners(0)
        for i in norm_order:
            norm(i)
        scale_out(1)
        scale_out(2)
        mix(0)
        nc.vector.tensor_scalar(hid[:, 0, :], staged[0][:], rstd[0][:], gain[0][:], ALU.mult, ALU.mult)
        nc.sync.dma_start(out=hid[lower, 1, :], in_=hid[upper, 0, :])
        nc.vector.tensor_copy(
            out=w2_bf[:].rearrange("p (a c t) -> p a t c", c=RUN, t=PACK),
            in_=w2_raw[:].rearrange("p t (a c) -> p a t c", c=RUN),
        )
        fetch_partners(1)
        scale_out(3)
        mix(1)
        nc.sync.dma_start(out=hid[upper, 0, :], in_=staged[1][lower, :])
        nc.sync.dma_start(out=hid[upper, 1, :], in_=staged[1][upper, :])
        quantise(w2_codes[:], w2_scales[:], w2_bf[:])
        for i in (2, 3):
            fetch_partners(i)
            mix(i)

        hid_bf = tiles("hid_bf", 2, [P, HALF_S * PACK], BF16)
        hid_codes = tiles("hid_codes", 2, [P, HALF_S], U32)
        hid_scales = tiles("hid_scales", 2, [P, HALF_S], U8)
        result = tiles("result", 2, [P, HALF_S], F32)
        acc = [ps.tile([P, HALF_S], F32, name=f"acc{u}") for u in range(2)]

        def interleave(copy, u, start, stop):
            copy(
                out=hid_bf[u][:, PACK * start : PACK * stop].rearrange("p (a c t) -> p a t c", c=RUN, t=PACK),
                in_=hid[:, :, u * HALF_S + start : u * HALF_S + stop].rearrange("p t (a c) -> p a t c", c=RUN),
            )

        interleave(nc.scalar.copy, 0, 0, SCALAR_TOKENS)
        interleave(nc.vector.tensor_copy, 1, 0, HALF_S)
        interleave(nc.vector.tensor_copy, 0, SCALAR_TOKENS, HALF_S)
        for u in (1, 0):
            quantise(hid_codes[u][:], hid_scales[u][:], hid_bf[u][:])
            nc.tensor.matmul_mx(
                out=acc[u][:],
                lhsT=w2_codes[:].bitcast(FP8X4),
                lhsT_scale=w2_scales[:],
                rhs=hid_codes[u][:].bitcast(FP8X4),
                rhs_scale=hid_scales[u][:],
                start=True,
                stop=True,
            )
        for u, copy in ((1, nc.scalar.copy), (0, nc.vector.tensor_copy)):
            copy(out=result[u][:], in_=acc[u][:])
            nc.sync.dma_start(out=out[:, halves[u]], in_=result[u][:])
